import numpy as np, ml_dtypes
CORES = [2,34,66,98,130,162,194,226,258,290,322,354,386,418,450,482]
N = 16
GR, GC, TK = 8, 2, 128
RA = [[1,-2,2,1,1,-1,1,-2],[-1,-2,-2,-2,-1,1,-1,2],[-2,-1,1,1,2,1,2,-2],[1,1,2,-2,1,2,-2,-1],[2,2,2,-1,-2,-1,1,-1],[-1,2,-2,-2,-1,1,-1,2],[2,2,-1,1,2,-1,-2,-1],[2,-1,2,2,-2,1,2,-1]]
CB = [[2,-1],[-1,-1]]
def setup_inputs(rng):
    return {"x": rng.standard_normal((N, 128, TK), dtype=np.float32).astype(ml_dtypes.bfloat16), "a": (rng.standard_normal((N, 128, 128), dtype=np.float32) / 11).astype(ml_dtypes.bfloat16)}
def setup_inputs_big(rng):
    d = setup_inputs(rng)
    for k in ("x", "a"): d[k] = (d[k].astype(np.float32) * 1024.0).astype(d[k].dtype)
    return d
def setup_inputs_small(rng):
    d = setup_inputs(rng)
    for k in ("x", "a"): d[k] = (d[k].astype(np.float32) * (1 / 1024.0)).astype(d[k].dtype)
    return d
def setup_inputs_apart(rng):
    d = setup_inputs(rng)
    f = (10.0 ** rng.permutation(np.linspace(-1.5, 1.5, N))).astype(np.float32).reshape(N, 1, 1)
    for k in ("x", "a"): d[k] = (d[k].astype(np.float32) * f).astype(d[k].dtype)
    return d
def reference(x, a):
    X, A = x.astype(np.float64), a.astype(np.float64)
    y = np.zeros((N, 128, TK))
    for i in range(GR):
        for j in range(GC):
            t = sum(RA[i][k] * CB[j][l] * X[k * GC + l] for k in range(GR) for l in range(GC))
            y[i * GC + j] = A[i * GC + j].T @ t
    return {"y": y.astype(ml_dtypes.bfloat16)}

@@ -1,0 +1,160 @@
+from concourse.bass import DstId, RemoteDMATransfer
+from concourse.mybir import AluOpType
+
+B = 128
+NV = 4
+NS = 4
+
+SCRATCH = {
+    "xg": ("sbuf", [B, NS * B], "bfloat16"),
+    "asb": ("sbuf", [B, B], "bfloat16"),
+    "cb": ("sbuf", [B, 2 * B], "bfloat16"),
+    "av": ("sbuf", [B, 2 * B], "bfloat16"),
+    "esrc": ("sbuf", [B, NV * B + 1], "bfloat16"),
+    "skew": ("dram", [B * (NV * B + 1)], "bfloat16"),
+    "eye": ("sbuf", [B, NV * B], "bfloat16"),
+    "qs": ("sbuf", [B, 4 * B], "bfloat16"),
+    "ql": ("sbuf", [B, 3 * B], "bfloat16"),
+    "ysb": ("sbuf", [B, B], "bfloat16"),
+    "ps0": ("psum", [B, 512], "float32"),
+    "ps1": ("psum", [B, 512], "float32"),
+    "ps2": ("psum", [B, 512], "float32"),
+    "ps3": ("psum", [B, 512], "float32"),
+    "psy": ("psum", [B, 512], "float32"),
+}
+SEMAPHORES = (["sx", "sa", "sz", "sms", "sd", "seye", "scb", "sav", "l1", "l2", "sy", "syc", "sst"]
+              + ["h1_%d" % i for i in range(NS)] + ["p%d" % i for i in range(4)]
+              + ["c%d" % i for i in range(4)] + ["h2_%d" % i for i in range(3)])
+
+
+def _bits(mask):
+    return [1 << e for e in range(mask.bit_length()) if mask >> e & 1]
+
+
+def _blk(t, i):
+    return t[:, i * B:(i + 1) * B]
+
+
+def rank_program(g, core, T, topo):
+    rank = T.rank_of(core)
+    if rank is None:
+        return
+    RA, CB, cores, S = T.tables["RA"], T.tables["CB"], T.cores, T.sem
+    n, gc = len(cores), len(CB)
+
+    def row(r):
+        return r // gc
+
+    def col(r):
+        return r % gc
+
+    def rack(r):
+        return topo.rack(topo.host(cores[r]))
+
+    def partner(r):
+        return row(r) * gc + (1 - col(r))
+
+    def cabled(r):
+        return [s for s in range(n) if rack(s) != rack(r) and topo.may_write(cores[r], cores[s])
+                and topo.chip(cores[s]) == topo.chip(cores[r])][0]
+
+    def dst_of(r):
+        rid, pid = topo.addr(cores[r], core)
+        return DstId(rid=rid, pnc=pid)
+
+    j = col(rank)
+    mem = [s for s in range(n) if col(s) == j and rack(s) == rack(rank)]
+    m = mem.index(rank)
+    vals = sorted(set(v for r in RA for v in r))
+    nv = len(vals)
+    sends = [(2, partner(cabled(rank))), (1, cabled(rank)), (0, partner(rank))]
+    made = [d for _, d in sends] + [rank]
+    land_col = [1 - j, j, 1 - j]
+
+    g.sync.dma_start(_blk(T.xg, m), T.x[:, :]).then_inc(S.sx, 16)
+    g.sync.wait_ge(S.sx, 16)
+    g.sync.dma_start(T.asb[:, :], T.a[:, :]).then_inc(S.sa, 16)
+
+    w = nv * B + 1
+    g.vector.memset(T.esrc[:, 0:w], 0.0).then_inc(S.sz, 1)
+    g.vector.wait_ge(S.sz, 1)
+    for v, c in enumerate(vals):
+        g.vector.memset(T.esrc[:, v * B:v * B + 1], float(c)).then_inc(S.sms, 1)
+    cvals = sorted(set(CB[j]))
+    for i, c in enumerate(cvals):
+        g.vector.memset(_blk(T.cb, i), float(c)).then_inc(S.scb, 1)
+
+    g.scalar.wait_ge(S.sms, nv)
+    g.scalar.dma_start(T.skew[0:B * w], T.esrc[:, 0:w]).then_inc(S.sd, 16)
+    g.scalar.wait_ge(S.sd, 16)
+    g.scalar.dma_start(T.eye[:, 0:nv * B], T.skew[0:B * nv * B]).then_inc(S.seye, 16)
+
+    g.vector.wait_ge(S.scb, len(cvals))
+    g.vector.wait_ge(S.sa, 16)
+    for i in range(len(cvals)):
+        g.vector.tensor_tensor(_blk(T.av, i), T.asb[:, :], _blk(T.cb, i), AluOpType.mult).then_inc(S.sav, 1)
+
+    peers = [mem[(m + d) % NS] for d in range(1, NS)]
+    mask1 = topo.mask(core, cores[peers[0]])
+    for p in peers:
+        mask1 &= topo.mask(core, cores[p])
+    n1 = len(_bits(mask1))
+    g.wait_ge(S.sx, 16)
+    g.remote_dma_fused([RemoteDMATransfer(dst_ids=[dst_of(p) for p in peers], dma_engine_mask=mask1,
+                                          remote_sem=S["h1_%d" % m], srcs=[_blk(T.xg, m)],
+                                          dsts=[_blk(T.xg, m) for _ in peers], alu_op=0)], local_sem=S.l1)
+
+    ps = [T.ps0, T.ps1, T.ps2, T.ps3]
+    order = [(m - d) % NS for d in range(NS)]
+    g.tensor.wait_ge(S.seye, 16)
+    g.tensor.wait_ge(S.sx, 16)
+    for k, s in enumerate(order):
+        if k:
+            g.tensor.wait_ge(S["h1_%d" % s], n1)
+        for i in range(3):
+            c = RA[row(made[i])][row(mem[s])]
+            mm = g.tensor.matmul(ps[i][:, 0:B], _blk(T.eye, vals.index(c)), _blk(T.xg, s), k == 0, k == NS - 1)
+            if k == NS - 1:
+                mm.then_inc(S["p%d" % i], 1)
+    for k, s in enumerate(order):
+        c = RA[row(rank)][row(mem[s])]
+        mm = g.tensor.matmul(ps[3][:, 0:B], _blk(T.eye, vals.index(c)), _blk(T.xg, s), k == 0, k == NS - 1)
+        if k == NS - 1:
+            mm.then_inc(S.p3, 1)
+
+    for i in range(4):
+        g.vector.wait_ge(S["p%d" % i], 1)
+        g.vector.tensor_copy(_blk(T.qs, i), ps[i][:, 0:B]).then_inc(S["c%d" % i], 1)
+
+    slot, d = sends[0]
+    rid, pid = topo.addr(cores[d], core)
+    mask_c = topo.mask(core, cores[d])
+    g.wait_ge(S.c0, 1)
+    g.remote_dma(out_ap=_blk(T.ql, slot), in_ap=_blk(T.qs, 0), remote_sem=S["h2_%d" % slot], local_sem=S.l2,
+                 pid=pid, routing_id=rid, dma_engine_mask=mask_c)
+    both = _bits(topo.mask(core, cores[sends[1][1]]) & topo.mask(core, cores[sends[2][1]]))
+    half = len(both) // 2
+    parts = [sum(both[:half]), sum(both[half:])]
+    g.wait_ge(S.c1, 1)
+    g.wait_ge(S.c2, 1)
+    g.remote_dma_fused([RemoteDMATransfer(dst_ids=[dst_of(sends[i][1])], dma_engine_mask=parts[i - 1],
+                                          remote_sem=S["h2_%d" % sends[i][0]], src=_blk(T.qs, i),
+                                          dst=_blk(T.ql, sends[i][0]), alu_op=0) for i in (1, 2)], local_sem=S.l2)
+
+    got = {2: len(_bits(mask_c)), 1: half, 0: half}
+    g.tensor.wait_ge(S.sav, len(cvals))
+    g.tensor.wait_ge(S.c3, 1)
+    g.tensor.matmul(T.psy[:, 0:B], _blk(T.av, cvals.index(CB[j][j])), _blk(T.qs, 3), True, False)
+    for k, slot in enumerate((2, 1, 0)):
+        g.tensor.wait_ge(S["h2_%d" % slot], got[slot])
+        mm = g.tensor.matmul(T.psy[:, 0:B], _blk(T.av, cvals.index(CB[j][land_col[slot]])), _blk(T.ql, slot),
+                             False, k == 2)
+    mm.then_inc(S.sy, 1)
+    g.vector.wait_ge(S.sy, 1)
+    g.vector.tensor_copy(T.ysb[:, :], T.psy[:, 0:B]).then_inc(S.syc, 1)
+    g.sync.wait_ge(S.syc, 1)
+    g.sync.dma_start(T.y[:, :], T.ysb[:, :]).then_inc(S.sst, 16)
+    g.sync.wait_ge(S.sst, 16)
+
+    g.wait_ge(S.l1, n1)
+    g.wait_ge(S.l2, len(_bits(mask_c)) + 2 * half)

@@ -2,29 +2,27 @@ from concourse.bass import DstId, RemoteDMATransfer
 from concourse.mybir import AluOpType
 
 B = 128
-NV = 4
+H = B // 2
+NE = 6
 NS = 4
 
 SCRATCH = {
+    "xs": ("dram", [B, B], "bfloat16"),
     "xg": ("sbuf", [B, NS * B], "bfloat16"),
     "asb": ("sbuf", [B, B], "bfloat16"),
-    "cb": ("sbuf", [B, 2 * B], "bfloat16"),
-    "av": ("sbuf", [B, 2 * B], "bfloat16"),
-    "esrc": ("sbuf", [B, NV * B + 1], "bfloat16"),
-    "skew": ("dram", [B * (NV * B + 1)], "bfloat16"),
-    "eye": ("sbuf", [B, NV * B], "bfloat16"),
-    "qs": ("sbuf", [B, 4 * B], "bfloat16"),
+    "av": ("sbuf", [B, 4 * B], "bfloat16"),
+    "pmi": ("sbuf", [B, B], "bfloat16"),
+    "eye": ("sbuf", [B, NE * B], "bfloat16"),
+    "qs": ("sbuf", [B, 2 * B], "bfloat16"),
     "ql": ("sbuf", [B, 3 * B], "bfloat16"),
     "ysb": ("sbuf", [B, B], "bfloat16"),
     "ps0": ("psum", [B, 512], "float32"),
     "ps1": ("psum", [B, 512], "float32"),
-    "ps2": ("psum", [B, 512], "float32"),
-    "ps3": ("psum", [B, 512], "float32"),
-    "psy": ("psum", [B, 512], "float32"),
+    "psy0": ("psum", [B, 512], "float32"),
+    "psy1": ("psum", [B, 512], "float32"),
 }
-SEMAPHORES = (["sx", "sa", "sz", "sms", "sd", "seye", "scb", "sav", "l1", "l2", "sy", "syc", "sst"]
-              + ["h1_%d" % i for i in range(NS)] + ["p%d" % i for i in range(4)]
-              + ["c%d" % i for i in range(4)] + ["h2_%d" % i for i in range(3)])
+SEMAPHORES = (["sxs", "sx", "sa", "sio", "seye", "sav", "l1", "l2", "sy0", "sy1", "syc", "sst", "p0", "p1", "c0", "c1"]
+              + ["h1_%d" % i for i in range(NS)] + ["h2_%d" % i for i in range(3)])
 
 
 def _bits(mask):
@@ -58,101 +56,120 @@ def rank_program(g, core, T, topo):
         return [s for s in range(n) if rack(s) != rack(r) and topo.may_write(cores[r], cores[s])
                 and topo.chip(cores[s]) == topo.chip(cores[r])][0]
 
+    def mem_of(r):
+        return [s for s in range(n) if col(s) == col(r) and rack(s) == rack(r)]
+
+    def last_of(r):
+        mm = mem_of(r)
+        return mm[(mm.index(r) - (NS - 1)) % NS]
+
+    def c_last(s, d):
+        return RA[row(d)][row(last_of(s))]
+
     def dst_of(r):
         rid, pid = topo.addr(cores[r], core)
         return DstId(rid=rid, pnc=pid)
 
     j = col(rank)
-    mem = [s for s in range(n) if col(s) == j and rack(s) == rack(rank)]
+    mem = mem_of(rank)
     m = mem.index(rank)
-    vals = sorted(set(v for r in RA for v in r))
-    nv = len(vals)
-    sends = [(2, partner(cabled(rank))), (1, cabled(rank)), (0, partner(rank))]
-    made = [d for _, d in sends] + [rank]
-    land_col = [1 - j, j, 1 - j]
+    order = [(m - d) % NS for d in range(NS)]
+    early, last = order[:NS - 1], order[NS - 1]
+    sum_row = [row(cabled(rank)), row(rank)]
+    ratio = [[RA[r][row(mem[s])] / RA[r][row(mem[last])] for s in early] for r in sum_row]
+    rvals = sorted(set(v for rr in ratio for v in rr))
+    terms = [(rank, T.qs, 1), (cabled(partner(rank)), T.ql, 2), (cabled(rank), T.ql, 1), (partner(rank), T.ql, 0)]
+    fac = [CB[j][col(t[0])] * c_last(t[0], rank) for t in terms]
+    fvals = sorted(set(fac))
 
+    g.sync.dma_start(T.xs[:, :], T.x[:, :]).then_inc(S.sxs, 16)
     g.sync.dma_start(_blk(T.xg, m), T.x[:, :]).then_inc(S.sx, 16)
-    g.sync.wait_ge(S.sx, 16)
     g.sync.dma_start(T.asb[:, :], T.a[:, :]).then_inc(S.sa, 16)
 
-    w = nv * B + 1
-    g.vector.memset(T.esrc[:, 0:w], 0.0).then_inc(S.sz, 1)
-    g.vector.wait_ge(S.sz, 1)
-    for v, c in enumerate(vals):
-        g.vector.memset(T.esrc[:, v * B:v * B + 1], float(c)).then_inc(S.sms, 1)
-    cvals = sorted(set(CB[j]))
-    for i, c in enumerate(cvals):
-        g.vector.memset(_blk(T.cb, i), float(c)).then_inc(S.scb, 1)
+    g.iota(T.pmi[:, :], [[-1, B]], 0, 1, allow_small_or_imprecise_dtypes=True).then_inc(S.sio, 1)
 
-    g.scalar.wait_ge(S.sms, nv)
-    g.scalar.dma_start(T.skew[0:B * w], T.esrc[:, 0:w]).then_inc(S.sd, 16)
-    g.scalar.wait_ge(S.sd, 16)
-    g.scalar.dma_start(T.eye[:, 0:nv * B], T.skew[0:B * nv * B]).then_inc(S.seye, 16)
-
-    g.vector.wait_ge(S.scb, len(cvals))
+    g.vector.wait_ge(S.sio, 1)
+    for v, c in enumerate(rvals):
+        g.vector.tensor_scalar(_blk(T.eye, v), T.pmi[:, :], 0.0, float(c), AluOpType.is_equal,
+                               AluOpType.mult).then_inc(S.seye, 1)
     g.vector.wait_ge(S.sa, 16)
-    for i in range(len(cvals)):
-        g.vector.tensor_tensor(_blk(T.av, i), T.asb[:, :], _blk(T.cb, i), AluOpType.mult).then_inc(S.sav, 1)
+    for v, c in enumerate(fvals):
+        g.vector.tensor_scalar(_blk(T.av, v), T.asb[:, :], float(c), None, AluOpType.mult).then_inc(S.sav, 1)
 
     peers = [mem[(m + d) % NS] for d in range(1, NS)]
     mask1 = topo.mask(core, cores[peers[0]])
     for p in peers:
         mask1 &= topo.mask(core, cores[p])
     n1 = len(_bits(mask1))
-    g.wait_ge(S.sx, 16)
+    g.wait_ge(S.sxs, 16)
     g.remote_dma_fused([RemoteDMATransfer(dst_ids=[dst_of(p) for p in peers], dma_engine_mask=mask1,
-                                          remote_sem=S["h1_%d" % m], srcs=[_blk(T.xg, m)],
+                                          remote_sem=S["h1_%d" % m], srcs=[T.xs[:, :]],
                                           dsts=[_blk(T.xg, m) for _ in peers], alu_op=0)], local_sem=S.l1)
 
-    ps = [T.ps0, T.ps1, T.ps2, T.ps3]
-    order = [(m - d) % NS for d in range(NS)]
-    g.tensor.wait_ge(S.seye, 16)
+    ps = [T.ps0, T.ps1]
+    ne = len(early)
+
+    def p_step(i, k):
+        mm = g.tensor.matmul(ps[i][:, 0:B], _blk(T.eye, rvals.index(ratio[i][k])), _blk(T.xg, early[k]),
+                             k == 0, k == ne - 1)
+        if k == ne - 1:
+            mm.then_inc(S["p%d" % i], 1)
+
+    g.tensor.wait_ge(S.seye, len(rvals))
     g.tensor.wait_ge(S.sx, 16)
-    for k, s in enumerate(order):
-        if k:
-            g.tensor.wait_ge(S["h1_%d" % s], n1)
-        for i in range(3):
-            c = RA[row(made[i])][row(mem[s])]
-            mm = g.tensor.matmul(ps[i][:, 0:B], _blk(T.eye, vals.index(c)), _blk(T.xg, s), k == 0, k == NS - 1)
-            if k == NS - 1:
-                mm.then_inc(S["p%d" % i], 1)
-    for k, s in enumerate(order):
-        c = RA[row(rank)][row(mem[s])]
-        mm = g.tensor.matmul(ps[3][:, 0:B], _blk(T.eye, vals.index(c)), _blk(T.xg, s), k == 0, k == NS - 1)
-        if k == NS - 1:
-            mm.then_inc(S.p3, 1)
+    p_step(0, 0)
+    p_step(1, 0)
+    for k in range(1, ne):
+        g.tensor.wait_ge(S["h1_%d" % early[k]], n1)
+        p_step(0, k)
+    for k in range(1, ne):
+        p_step(1, k)
 
-    for i in range(4):
+    g.vector.wait_ge(S["h1_%d" % last], n1)
+    for i in range(2):
         g.vector.wait_ge(S["p%d" % i], 1)
-        g.vector.tensor_copy(_blk(T.qs, i), ps[i][:, 0:B]).then_inc(S["c%d" % i], 1)
+        g.vector.tensor_tensor(_blk(T.qs, i), ps[i][:, 0:B], _blk(T.xg, last), AluOpType.add).then_inc(S["c%d" % i], 1)
 
-    slot, d = sends[0]
-    rid, pid = topo.addr(cores[d], core)
-    mask_c = topo.mask(core, cores[d])
+    d_c, d_b, d_a = partner(cabled(rank)), cabled(rank), partner(rank)
+    rid, pid = topo.addr(cores[d_c], core)
+    mask_c = topo.mask(core, cores[d_c])
     g.wait_ge(S.c0, 1)
-    g.remote_dma(out_ap=_blk(T.ql, slot), in_ap=_blk(T.qs, 0), remote_sem=S["h2_%d" % slot], local_sem=S.l2,
+    g.remote_dma(out_ap=_blk(T.ql, 2), in_ap=_blk(T.qs, 0), remote_sem=S.h2_2, local_sem=S.l2,
                  pid=pid, routing_id=rid, dma_engine_mask=mask_c)
-    both = _bits(topo.mask(core, cores[sends[1][1]]) & topo.mask(core, cores[sends[2][1]]))
+    both = _bits(topo.mask(core, cores[d_b]) & topo.mask(core, cores[d_a]))
     half = len(both) // 2
-    parts = [sum(both[:half]), sum(both[half:])]
     g.wait_ge(S.c1, 1)
-    g.wait_ge(S.c2, 1)
-    g.remote_dma_fused([RemoteDMATransfer(dst_ids=[dst_of(sends[i][1])], dma_engine_mask=parts[i - 1],
-                                          remote_sem=S["h2_%d" % sends[i][0]], src=_blk(T.qs, i),
-                                          dst=_blk(T.ql, sends[i][0]), alu_op=0) for i in (1, 2)], local_sem=S.l2)
+    g.remote_dma_fused([RemoteDMATransfer(dst_ids=[dst_of(d_b)], dma_engine_mask=sum(both[0::2]), remote_sem=S.h2_1,
+                                          src=_blk(T.qs, 0), dst=_blk(T.ql, 1), alu_op=0),
+                        RemoteDMATransfer(dst_ids=[dst_of(d_a)], dma_engine_mask=sum(both[1::2]), remote_sem=S.h2_0,
+                                          src=_blk(T.qs, 1), dst=_blk(T.ql, 0), alu_op=0)], local_sem=S.l2)
 
-    got = {2: len(_bits(mask_c)), 1: half, 0: half}
-    g.tensor.wait_ge(S.sav, len(cvals))
-    g.tensor.wait_ge(S.c3, 1)
-    g.tensor.matmul(T.psy[:, 0:B], _blk(T.av, cvals.index(CB[j][j])), _blk(T.qs, 3), True, False)
-    for k, slot in enumerate((2, 1, 0)):
-        g.tensor.wait_ge(S["h2_%d" % slot], got[slot])
-        mm = g.tensor.matmul(T.psy[:, 0:B], _blk(T.av, cvals.index(CB[j][land_col[slot]])), _blk(T.ql, slot),
-                             False, k == 2)
-    mm.then_inc(S.sy, 1)
-    g.vector.wait_ge(S.sy, 1)
-    g.vector.tensor_copy(T.ysb[:, :], T.psy[:, 0:B]).then_inc(S.syc, 1)
-    g.sync.wait_ge(S.syc, 1)
+    psy = [T.psy0, T.psy1]
+    nt = len(terms)
+
+    def y_step(k, h):
+        s, buf, b = terms[k]
+        mm = g.tensor.matmul(psy[h][:, 0:H], _blk(T.av, fvals.index(fac[k])),
+                             buf[:, b * B + h * H:b * B + (h + 1) * H], k == 0, k == nt - 1)
+        if k == nt - 1:
+            mm.then_inc(S["sy%d" % h], 1)
+
+    g.tensor.wait_ge(S.sav, len(fvals))
+    g.tensor.wait_ge(S.c1, 1)
+    y_step(0, 0)
+    y_step(0, 1)
+    g.tensor.wait_ge(S.h2_2, len(_bits(mask_c)))
+    y_step(1, 0)
+    y_step(1, 1)
+    g.tensor.wait_ge(S.h2_1, half)
+    g.tensor.wait_ge(S.h2_0, half)
+    for h in range(2):
+        y_step(2, h)
+        y_step(3, h)
+    for h in range(2):
+        g.vector.wait_ge(S["sy%d" % h], 1)
+        g.vector.tensor_copy(T.ysb[:, h * H:(h + 1) * H], psy[h][:, 0:H]).then_inc(S.syc, 1)
+    g.sync.wait_ge(S.syc, 2)
     g.sync.dma_start(T.y[:, :], T.ysb[:, :]).then_inc(S.sst, 16)
     g.sync.wait_ge(S.sst, 16)
 

from concourse.bass import DstId, RemoteDMATransfer
from concourse.mybir import AluOpType

B = 128
H = B // 2
NE = 6
NS = 4

SCRATCH = {
    "xs": ("dram", [B, B], "bfloat16"),
    "xg": ("sbuf", [B, NS * B], "bfloat16"),
    "asb": ("sbuf", [B, B], "bfloat16"),
    "av": ("sbuf", [B, 4 * B], "bfloat16"),
    "pmi": ("sbuf", [B, B], "bfloat16"),
    "eye": ("sbuf", [B, NE * B], "bfloat16"),
    "qs": ("sbuf", [B, 2 * B], "bfloat16"),
    "ql": ("sbuf", [B, 3 * B], "bfloat16"),
    "ysb": ("sbuf", [B, B], "bfloat16"),
    "ps0": ("psum", [B, 512], "float32"),
    "ps1": ("psum", [B, 512], "float32"),
    "psy0": ("psum", [B, 512], "float32"),
    "psy1": ("psum", [B, 512], "float32"),
}
SEMAPHORES = (["sxs", "sx", "sa", "sio", "seye", "sav", "l1", "l2", "sy0", "sy1", "syc", "sst", "p0", "p1", "c0", "c1"]
              + ["h1_%d" % i for i in range(NS)] + ["h2_%d" % i for i in range(3)])


def _bits(mask):
    return [1 << e for e in range(mask.bit_length()) if mask >> e & 1]


def _blk(t, i):
    return t[:, i * B:(i + 1) * B]


def rank_program(g, core, T, topo):
    rank = T.rank_of(core)
    if rank is None:
        return
    RA, CB, cores, S = T.tables["RA"], T.tables["CB"], T.cores, T.sem
    n, gc = len(cores), len(CB)

    def row(r):
        return r // gc

    def col(r):
        return r % gc

    def rack(r):
        return topo.rack(topo.host(cores[r]))

    def partner(r):
        return row(r) * gc + (1 - col(r))

    def cabled(r):
        return [s for s in range(n) if rack(s) != rack(r) and topo.may_write(cores[r], cores[s])
                and topo.chip(cores[s]) == topo.chip(cores[r])][0]

    def mem_of(r):
        return [s for s in range(n) if col(s) == col(r) and rack(s) == rack(r)]

    def last_of(r):
        mm = mem_of(r)
        return mm[(mm.index(r) - (NS - 1)) % NS]

    def c_last(s, d):
        return RA[row(d)][row(last_of(s))]

    def dst_of(r):
        rid, pid = topo.addr(cores[r], core)
        return DstId(rid=rid, pnc=pid)

    j = col(rank)
    mem = mem_of(rank)
    m = mem.index(rank)
    order = [(m - d) % NS for d in range(NS)]
    early, last = order[:NS - 1], order[NS - 1]
    sum_row = [row(cabled(rank)), row(rank)]
    ratio = [[RA[r][row(mem[s])] / RA[r][row(mem[last])] for s in early] for r in sum_row]
    rvals = sorted(set(v for rr in ratio for v in rr))
    terms = [(rank, T.qs, 1), (cabled(partner(rank)), T.ql, 2), (cabled(rank), T.ql, 1), (partner(rank), T.ql, 0)]
    fac = [CB[j][col(t[0])] * c_last(t[0], rank) for t in terms]
    fvals = sorted(set(fac))

    g.sync.dma_start(T.xs[:, :], T.x[:, :]).then_inc(S.sxs, 16)
    g.sync.dma_start(_blk(T.xg, m), T.x[:, :]).then_inc(S.sx, 16)
    g.sync.dma_start(T.asb[:, :], T.a[:, :]).then_inc(S.sa, 16)

    g.iota(T.pmi[:, :], [[-1, B]], 0, 1, allow_small_or_imprecise_dtypes=True).then_inc(S.sio, 1)

    g.vector.wait_ge(S.sio, 1)
    for v, c in enumerate(rvals):
        g.vector.tensor_scalar(_blk(T.eye, v), T.pmi[:, :], 0.0, float(c), AluOpType.is_equal,
                               AluOpType.mult).then_inc(S.seye, 1)
    g.vector.wait_ge(S.sa, 16)
    for v, c in enumerate(fvals):
        g.vector.tensor_scalar(_blk(T.av, v), T.asb[:, :], float(c), None, AluOpType.mult).then_inc(S.sav, 1)

    peers = [mem[(m + d) % NS] for d in range(1, NS)]
    mask1 = topo.mask(core, cores[peers[0]])
    for p in peers:
        mask1 &= topo.mask(core, cores[p])
    n1 = len(_bits(mask1))
    g.wait_ge(S.sxs, 16)
    g.remote_dma_fused([RemoteDMATransfer(dst_ids=[dst_of(p) for p in peers], dma_engine_mask=mask1,
                                          remote_sem=S["h1_%d" % m], srcs=[T.xs[:, :]],
                                          dsts=[_blk(T.xg, m) for _ in peers], alu_op=0)], local_sem=S.l1)

    ps = [T.ps0, T.ps1]
    ne = len(early)

    def p_step(i, k):
        mm = g.tensor.matmul(ps[i][:, 0:B], _blk(T.eye, rvals.index(ratio[i][k])), _blk(T.xg, early[k]),
                             k == 0, k == ne - 1)
        if k == ne - 1:
            mm.then_inc(S["p%d" % i], 1)

    g.tensor.wait_ge(S.seye, len(rvals))
    g.tensor.wait_ge(S.sx, 16)
    p_step(0, 0)
    p_step(1, 0)
    for k in range(1, ne):
        g.tensor.wait_ge(S["h1_%d" % early[k]], n1)
        p_step(0, k)
    for k in range(1, ne):
        p_step(1, k)

    g.vector.wait_ge(S["h1_%d" % last], n1)
    for i in range(2):
        g.vector.wait_ge(S["p%d" % i], 1)
        g.vector.tensor_tensor(_blk(T.qs, i), ps[i][:, 0:B], _blk(T.xg, last), AluOpType.add).then_inc(S["c%d" % i], 1)

    d_c, d_b, d_a = partner(cabled(rank)), cabled(rank), partner(rank)
    rid, pid = topo.addr(cores[d_c], core)
    mask_c = topo.mask(core, cores[d_c])
    g.wait_ge(S.c0, 1)
    g.remote_dma(out_ap=_blk(T.ql, 2), in_ap=_blk(T.qs, 0), remote_sem=S.h2_2, local_sem=S.l2,
                 pid=pid, routing_id=rid, dma_engine_mask=mask_c)
    both = _bits(topo.mask(core, cores[d_b]) & topo.mask(core, cores[d_a]))
    half = len(both) // 2
    g.wait_ge(S.c1, 1)
    g.remote_dma_fused([RemoteDMATransfer(dst_ids=[dst_of(d_b)], dma_engine_mask=sum(both[0::2]), remote_sem=S.h2_1,
                                          src=_blk(T.qs, 0), dst=_blk(T.ql, 1), alu_op=0),
                        RemoteDMATransfer(dst_ids=[dst_of(d_a)], dma_engine_mask=sum(both[1::2]), remote_sem=S.h2_0,
                                          src=_blk(T.qs, 1), dst=_blk(T.ql, 0), alu_op=0)], local_sem=S.l2)

    psy = [T.psy0, T.psy1]
    nt = len(terms)

    def y_step(k, h):
        s, buf, b = terms[k]
        mm = g.tensor.matmul(psy[h][:, 0:H], _blk(T.av, fvals.index(fac[k])),
                             buf[:, b * B + h * H:b * B + (h + 1) * H], k == 0, k == nt - 1)
        if k == nt - 1:
            mm.then_inc(S["sy%d" % h], 1)

    g.tensor.wait_ge(S.sav, len(fvals))
    g.tensor.wait_ge(S.c1, 1)
    y_step(0, 0)
    y_step(0, 1)
    g.tensor.wait_ge(S.h2_2, len(_bits(mask_c)))
    y_step(1, 0)
    y_step(1, 1)
    g.tensor.wait_ge(S.h2_1, half)
    g.tensor.wait_ge(S.h2_0, half)
    for h in range(2):
        y_step(2, h)
        y_step(3, h)
    for h in range(2):
        g.vector.wait_ge(S["sy%d" % h], 1)
        g.vector.tensor_copy(T.ysb[:, h * H:(h + 1) * H], psy[h][:, 0:H]).then_inc(S.syc, 1)
    g.sync.wait_ge(S.syc, 2)
    g.sync.dma_start(T.y[:, :], T.ysb[:, :]).then_inc(S.sst, 16)
    g.sync.wait_ge(S.sst, 16)

    g.wait_ge(S.l1, n1)
    g.wait_ge(S.l2, len(_bits(mask_c)) + 2 * half)
